import numpy as np
import ml_dtypes

BF16 = ml_dtypes.bfloat16


def bf(x):
    return np.asarray(x, np.float32).astype(BF16)


def f32(x):
    return np.asarray(x, np.float32)


def f64(x):
    return np.asarray(x).astype(np.float64)


def striped(idx):
    return np.tile(idx.reshape(-1, 16).T, (8, 1))


S, K, M, N, D, V = 256, 128, 512, 192, 8, 24


def setup_inputs():
    return {"table": bf(np.random.standard_normal((S, K))), "w": bf(np.random.standard_normal((K, M)) / np.sqrt(K)), "b": f32(0.5 * np.random.standard_normal((M, 1))), "offs": striped(np.random.permutation(np.tile(np.arange(S), 2))[:N])}


def reference(table, w, b, offs):
    idx = offs[:16].T.reshape(-1)
    x = f64(table)[idx].T
    y = f64(w).T @ x
    z = y + f64(b)
    return z.reshape(M, V, D).max(axis=2)

@@ -1,0 +1,59 @@
+import concourse.mybir as mybir
+from concourse.masks import make_identity
+
+BF16, F32, U16 = mybir.dt.bfloat16, mybir.dt.float32, mybir.dt.uint16
+add, maximum = mybir.AluOpType.add, mybir.AluOpType.max
+
+P = 128
+S, M, N = 256, 512, 192
+NEIGHBOURS = 8
+V = N // NEIGHBOURS
+NODE_BLOCKS = S // P
+M_BLOCKS = M // P
+
+FLOPS = 2 * P * M * N
+
+
+def tile_gather_matmul_kernel(tc, table, w, b, offs, out):
+    nc = tc.nc
+    with (
+        tc.tile_pool(name="held", bufs=1) as held,
+        tc.psum_pool(name="flip", bufs=1) as flip,
+        tc.psum_pool(name="products", bufs=1) as products,
+    ):
+        nodes = held.tile([P, NODE_BLOCKS, P], BF16, name="nodes")
+        offsets = held.tile([P, N // 16], U16, name="offsets")
+        weights = held.tile([P, M], BF16, name="weights")
+        bias = held.tile([P, M_BLOCKS], F32, name="bias")
+        nc.sync.dma_start(nodes[:], table.rearrange("(c p) k -> p c k", p=P))
+        nc.scalar.dma_start(weights[:], w)
+        nc.sync.dma_start(offsets[:], offs)
+        nc.scalar.dma_start(bias[:], b.rearrange("(p a) o -> p (a o)", a=M_BLOCKS))
+
+        identity = held.tile([P, P], BF16, name="identity")
+        make_identity(nc, identity[:])
+
+        flipped = flip.tile([P, S], BF16, name="flipped")
+        for c in range(NODE_BLOCKS):
+            nc.tensor.transpose(flipped[:, c * P : (c + 1) * P], nodes[:, c, :], identity[:])
+        window = held.tile([P, S], BF16, name="window")
+        nc.vector.tensor_copy(window[:], flipped[:])
+
+        weight_blocks = weights[:].rearrange("k (p a) -> k a p", a=M_BLOCKS)
+        pooled = held.tile([P, M_BLOCKS, V], F32, name="pooled")
+        for a in range(M_BLOCKS):
+            y = products.tile([P, N], F32, name=f"y{a}")
+            nc.tensor.matmul(
+                y[:], weight_blocks[:, a, :], window[:].indirect(offsets[:]), start=True, stop=True
+            )
+            nc.vector.tensor_reduce(
+                pooled[:, a, :],
+                y[:].rearrange("p (v t) -> p v t", t=NEIGHBOURS),
+                axis=mybir.AxisListType.X,
+                op=maximum,
+            )
+
+        result = held.tile([P, M_BLOCKS, V], F32, name="result")
+        bias_columns = bias[:].unsqueeze(2).to_broadcast([P, M_BLOCKS, V])
+        nc.vector.tensor_tensor(result[:], pooled[:], bias_columns, add)
+        nc.sync.dma_start(out.rearrange("(p a) v -> p a v", a=M_BLOCKS), result[:])

@@ -26,8 +26,8 @@ def tile_gather_matmul_kernel(tc, table, w, b, offs, out):
         weights = held.tile([P, M], BF16, name="weights")
         bias = held.tile([P, M_BLOCKS], F32, name="bias")
         nc.sync.dma_start(nodes[:], table.rearrange("(c p) k -> p c k", p=P))
-        nc.scalar.dma_start(weights[:], w)
         nc.sync.dma_start(offsets[:], offs)
+        nc.sync.dma_start(weights[:], w)
         nc.scalar.dma_start(bias[:], b.rearrange("(p a) o -> p (a o)", a=M_BLOCKS))
 
         identity = held.tile([P, P], BF16, name="identity")

@@ -33,11 +33,11 @@ def tile_gather_matmul_kernel(tc, table, w, b, offs, out):
         identity = held.tile([P, P], BF16, name="identity")
         make_identity(nc, identity[:])
 
-        flipped = flip.tile([P, S], BF16, name="flipped")
-        for c in range(NODE_BLOCKS):
-            nc.tensor.transpose(flipped[:, c * P : (c + 1) * P], nodes[:, c, :], identity[:])
         window = held.tile([P, S], BF16, name="window")
-        nc.vector.tensor_copy(window[:], flipped[:])
+        for c in range(NODE_BLOCKS):
+            flipped = flip.tile([P, P], BF16, name=f"flipped{c}")
+            nc.tensor.transpose(flipped[:], nodes[:, c, :], identity[:])
+            nc.vector.tensor_copy(window[:, c * P : (c + 1) * P], flipped[:])
 
         weight_blocks = weights[:].rearrange("k (p a) -> k a p", a=M_BLOCKS)
         pooled = held.tile([P, M_BLOCKS, V], F32, name="pooled")

import concourse.mybir as mybir
from concourse.masks import make_identity

BF16, F32, U16 = mybir.dt.bfloat16, mybir.dt.float32, mybir.dt.uint16
add, maximum = mybir.AluOpType.add, mybir.AluOpType.max

P = 128
S, M, N = 256, 512, 192
NEIGHBOURS = 8
V = N // NEIGHBOURS
NODE_BLOCKS = S // P
M_BLOCKS = M // P

FLOPS = 2 * P * M * N


def tile_gather_matmul_kernel(tc, table, w, b, offs, out):
    nc = tc.nc
    with (
        tc.tile_pool(name="held", bufs=1) as held,
        tc.psum_pool(name="flip", bufs=1) as flip,
        tc.psum_pool(name="products", bufs=1) as products,
    ):
        nodes = held.tile([P, NODE_BLOCKS, P], BF16, name="nodes")
        offsets = held.tile([P, N // 16], U16, name="offsets")
        weights = held.tile([P, M], BF16, name="weights")
        bias = held.tile([P, M_BLOCKS], F32, name="bias")
        nc.sync.dma_start(nodes[:], table.rearrange("(c p) k -> p c k", p=P))
        nc.sync.dma_start(offsets[:], offs)
        nc.sync.dma_start(weights[:], w)
        nc.scalar.dma_start(bias[:], b.rearrange("(p a) o -> p (a o)", a=M_BLOCKS))

        identity = held.tile([P, P], BF16, name="identity")
        make_identity(nc, identity[:])

        window = held.tile([P, S], BF16, name="window")
        for c in range(NODE_BLOCKS):
            flipped = flip.tile([P, P], BF16, name=f"flipped{c}")
            nc.tensor.transpose(flipped[:], nodes[:, c, :], identity[:])
            nc.vector.tensor_copy(window[:, c * P : (c + 1) * P], flipped[:])

        weight_blocks = weights[:].rearrange("k (p a) -> k a p", a=M_BLOCKS)
        pooled = held.tile([P, M_BLOCKS, V], F32, name="pooled")
        for a in range(M_BLOCKS):
            y = products.tile([P, N], F32, name=f"y{a}")
            nc.tensor.matmul(
                y[:], weight_blocks[:, a, :], window[:].indirect(offsets[:]), start=True, stop=True
            )
            nc.vector.tensor_reduce(
                pooled[:, a, :],
                y[:].rearrange("p (v t) -> p v t", t=NEIGHBOURS),
                axis=mybir.AxisListType.X,
                op=maximum,
            )

        result = held.tile([P, M_BLOCKS, V], F32, name="result")
        bias_columns = bias[:].unsqueeze(2).to_broadcast([P, M_BLOCKS, V])
        nc.vector.tensor_tensor(result[:], pooled[:], bias_columns, add)
        nc.sync.dma_start(out.rearrange("(p a) v -> p a v", a=M_BLOCKS), result[:])
